import numpy as np
import ml_dtypes


def mxq(x, axis, fmt="e4m3"):
    dtype, down = {"e4m3": (ml_dtypes.float8_e4m3fn, 7), "e5m2": (ml_dtypes.float8_e5m2, 14)}[fmt]
    v = np.moveaxis(np.asarray(x, np.float32).astype(ml_dtypes.bfloat16).astype(np.float64), axis, -1)
    blocks = v.reshape(v.shape[:-1] + (-1, 32))
    amax = np.abs(blocks).max(-1, keepdims=True)
    byte = np.maximum(np.where(amax > 0, np.frexp(amax)[1] - 1 + 127, 0) - down, 1)
    scale = np.exp2(byte - 127.0)
    codes = (blocks / scale).astype(np.float32).astype(dtype).astype(np.float64)
    return np.moveaxis((codes * scale).reshape(v.shape), -1, axis)


WIDE = False


def mx_kscale(k, group=512):
    if not WIDE:
        return np.ones(k)
    levels = np.array([10, -10, 5, -5, 0])
    if group != 512:
        return np.exp2(np.random.permutation(np.resize(levels, k // group))).repeat(group)
    if k % 512:
        return np.exp2(np.random.permutation(np.resize(levels, k // 32))).repeat(32)
    a = np.empty((k // 512, 16))
    for p in range(k // 512):
        a[p, :8] = np.random.permutation(np.resize(levels, 8))
        for g in range(8):
            far = levels[np.abs(levels - a[p, g]) >= 10]
            a[p, g + 8] = far[np.random.randint(len(far))]
    return np.exp2(a.ravel()).repeat(32)


def f64(x):
    return np.asarray(x).astype(np.float64)


H, D, N = 8, 256, 512


def setup_inputs():
    n = np.random.standard_normal
    s = mx_kscale(D, 0)[:, None]
    S = n((H, D, 128))
    S[:, :, 127] = np.random.uniform(0.5, 1.5, (H, D))
    return {
        "q": n((H, D, N)).astype(np.float32),
        "qa": (np.random.uniform(0.5, 2.0, (D, 1)) * s).astype(np.float32),
        "S": (S / s).astype(np.float32),
    }


def reference(q, qa, S):
    fq = (np.where(f64(q) > 0, f64(q) + 1.0, np.exp(np.minimum(f64(q), 0.0)))) * f64(qa)
    y = mxq(fq, 1, "e4m3").transpose(0, 2, 1) @ mxq(f64(S), 1, "e4m3")
    y = y / y[:, :, 127:128]
    return y

@@ -1,0 +1,215 @@
+from contextlib import ExitStack
+
+import concourse.mybir as mybir
+
+H, D, N, E = 8, 256, 512, 128
+FLOPS = 2 * H * N * D * E
+
+F32 = mybir.dt.float32
+BF16 = mybir.dt.bfloat16
+U32 = mybir.dt.uint32
+U8 = mybir.dt.uint8
+FP8X4 = mybir.dt.float8_e4m3fn_x4
+ACT = mybir.ActivationFunctionType
+ALU = mybir.AluOpType
+
+P = 128
+PACK = 4
+ROWS = D // PACK
+SIDE = P // ROWS
+PAIRS = H // SIDE
+M = 128
+RUN = 4
+
+
+def tile_rows_read_elu1_norm_kernel(tc, q, qa, S, out):
+    nc = tc.nc
+    q_hbm = q.rearrange("h (p j) n -> (h p) j n", j=PACK)
+    s_hbm = S.rearrange("h (p j) e -> (h p) j e", j=PACK)
+    qa_hbm = qa.rearrange("(p j) o -> p (j o)", j=PACK)
+
+    with ExitStack() as ctx:
+        sb = ctx.enter_context(tc.tile_pool(name="sb", bufs=1))
+        psum = ctx.enter_context(tc.psum_pool(name="psum", bufs=1))
+
+        def per_pair(name, shape, dtype):
+            return [sb.tile(shape, dtype, name="%s%d" % (name, g), align_bytes=64) for g in range(PAIRS)]
+
+        q_raw = per_pair("q_raw", [P, PACK, N], F32)
+        q_exp = per_pair("q_exp", [P, PACK, N], F32)
+        low = per_pair("low", [P, PACK, N], F32)
+        high = per_pair("high", [P, PACK, N], F32)
+        fq = per_pair("fq", [P, N, PACK], BF16)
+        q_codes = per_pair("q_codes", [P, N], U32)
+        q_scales = per_pair("q_scales", [P, N], U8)
+        s_raw = per_pair("s_raw", [P, PACK, E], F32)
+        s_bf = per_pair("s_bf", [P, E, PACK], BF16)
+        s_codes = per_pair("s_codes", [P, E], U32)
+        s_scales = per_pair("s_scales", [P, E], U8)
+        res = per_pair("res", [P, SIDE, N // M, E], F32)
+        weight = sb.tile([P, PACK], F32, name="weight")
+        zero = sb.tile([P, 1], F32, name="zero")
+        one = sb.tile([P, 1], F32, name="one")
+        banks = [[psum.tile([P, N // M, E], F32, name="bank%d_%d" % (c, b)) for b in range(4)] for c in range(SIDE)]
+
+        pieces = [(0, 0, 4, 0), (1, 0, 4, 1), (2, 0, 4, 2), (3, 0, 2, 3), (3, 2, 1, 0), (3, 3, 1, 1)]
+        inv = [[sb.tile([P, 8], F32, name="inv%d_%d" % (i, c)) for c in range(SIDE)] for i in range(len(pieces))]
+
+        def load_q(g, j0, j1):
+            nc.sync.dma_start(out=q_raw[g][:, j0:j1, :], in_=q_hbm[g * P : (g + 1) * P, j0:j1, :])
+
+        def load_s(g):
+            nc.sync.dma_start(out=s_raw[g][:], in_=s_hbm[g * P : (g + 1) * P, :, :])
+
+        def exp_q(g, j0, j1):
+            nc.scalar.activation(out=q_exp[g][:, j0:j1, :], in_=q_raw[g][:, j0:j1, :], func=ACT.Exp)
+
+        def make_high(g, j0, j1):
+            nc.vector.tensor_scalar(out=high[g][:, j0:j1, :], in0=q_raw[g][:, j0:j1, :], scalar1=0.0, scalar2=1.0, op0=ALU.max, op1=ALU.add)
+
+        def make_low(g, j, n0=0, n1=N):
+            nc.vector.tensor_scalar(out=low[g][:, j, n0:n1], in0=q_exp[g][:, j, n0:n1], scalar1=one[:, 0:1], scalar2=weight[:, j : j + 1], op0=ALU.min, op1=ALU.mult)
+
+        def runs(ap):
+            return ap.rearrange("p j (c i) -> p c j i", i=RUN)
+
+        def words(ap):
+            return ap.rearrange("p (c i) j -> p c j i", i=RUN)
+
+        def product(g, n0, n1):
+            nc.vector.tensor_tensor(out=words(fq[g][:, n0:n1, :]), in0=runs(low[g][:, :, n0:n1]), in1=runs(high[g][:, :, n0:n1]), op=ALU.mult)
+
+        def quant_q(g, n0, n1):
+            nc.vector.quantize_mx(out=q_codes[g][:, n0:n1].bitcast(FP8X4), scales=q_scales[g][:, n0:n1], in_=fq[g][:, n0:n1, :].rearrange("p n j -> p (n j)"))
+
+        def round_s(g):
+            nc.scalar.copy(out=words(s_bf[g][:]), in_=runs(s_raw[g][:]))
+
+        def quant_s(g):
+            nc.vector.quantize_mx(out=s_codes[g][:].bitcast(FP8X4), scales=s_scales[g][:], in_=s_bf[g][:].rearrange("p e j -> p (e j)"))
+
+        def multiply(i):
+            g, r0, nr, b = pieces[i]
+            for r in range(nr):
+                cols = slice((r0 + r) * M, (r0 + r + 1) * M)
+                for c in range(SIDE):
+                    rows = slice(c * ROWS, (c + 1) * ROWS)
+                    nc.tensor.matmul_mx(
+                        out=banks[c][b][:, r, :],
+                        lhsT=q_codes[g][rows, cols].bitcast(FP8X4),
+                        lhsT_scale=q_scales[g][rows, cols],
+                        rhs=s_codes[g][rows, :].bitcast(FP8X4),
+                        rhs_scale=s_scales[g][rows, :],
+                        start=True,
+                        stop=True,
+                    )
+
+        def invert(i, c):
+            g, r0, nr, b = pieces[i]
+            nc.vector.reciprocal(out=inv[i][c][:, 0:nr], in_=banks[c][b][:, 0:nr, E - 1])
+
+        def divide(i, c):
+            g, r0, nr, b = pieces[i]
+            for r in range(nr):
+                nc.scalar.activation(out=res[g][:, c, r0 + r, :], in_=banks[c][b][:, r, :], func=ACT.Copy, scale=inv[i][c][:, r : r + 1])
+
+        def divide_on_vector(i, c):
+            g, r0, nr, b = pieces[i]
+            for r in range(nr):
+                nc.vector.tensor_scalar(out=res[g][:, c, r0 + r, :], in0=banks[c][b][:, r, :], scalar1=inv[i][c][:, r : r + 1], scalar2=None, op0=ALU.mult)
+
+        def store(i, c):
+            g, r0, nr, b = pieces[i]
+            dst = out[g * SIDE + c].rearrange("(r s) e -> s r e", s=M)
+            nc.sync.dma_start(out=dst[:, r0 : r0 + nr, :], in_=res[g][:, c, r0 : r0 + nr, :])
+
+        def store_both(i):
+            g, r0, nr, b = pieces[i]
+            dst = out[g * SIDE : (g + 1) * SIDE, r0 * M : (r0 + 1) * M, :].rearrange("c s e -> s c e")
+            nc.sync.dma_start(out=dst, in_=res[g][:, :, r0, :])
+
+        with tc.manual_schedule():
+            for c in range(SIDE):
+                nc.scalar.dma_start(out=weight[c * ROWS : (c + 1) * ROWS, :], in_=qa_hbm)
+            for j in range(PACK):
+                load_q(0, j, j + 1)
+            load_q(1, 0, 2)
+            load_s(0)
+            load_q(1, 2, 4)
+            load_s(1)
+            for g in (2, 3):
+                load_q(g, 0, 2)
+                load_q(g, 2, 4)
+                load_s(g)
+
+            nc.vector.memset(zero[:], 0.0)
+            nc.scalar.activation(out=one[:], in_=zero[:], func=ACT.Exp)
+
+            for j in range(PACK):
+                exp_q(0, j, j + 1)
+                make_high(0, j, j + 1)
+                if j < PACK - 1:
+                    make_low(0, j)
+            make_low(0, PACK - 1, 0, N // 2)
+            make_low(0, PACK - 1, N // 2, N)
+            product(0, 0, N // 2)
+            product(0, N // 2, N)
+            exp_q(1, 0, 2)
+            round_s(0)
+            exp_q(1, 2, 4)
+            round_s(1)
+            make_high(1, 0, 2)
+            quant_q(0, 0, N)
+            make_high(1, 2, 4)
+            quant_s(0)
+            multiply(0)
+            for j in range(PACK):
+                make_low(1, j)
+            quant_s(1)
+            invert(0, 0)
+            invert(0, 1)
+
+            for g in (1, 2):
+                product(g, 0, N)
+                exp_q(g + 1, 0, 2)
+                exp_q(g + 1, 2, 4)
+                round_s(g + 1)
+                for c in range(SIDE):
+                    divide(g - 1, c)
+                    store(g - 1, c)
+                make_high(g + 1, 0, 4)
+                quant_q(g, 0, N)
+                multiply(g)
+                for j in range(PACK):
+                    make_low(g + 1, j)
+                quant_s(g + 1)
+                invert(g, 0)
+                invert(g, 1)
+
+            product(3, 0, 256)
+            for c in range(SIDE):
+                divide(2, c)
+                store(2, c)
+            product(3, 256, 384)
+            quant_q(3, 0, 256)
+            multiply(3)
+            product(3, 384, 512)
+            quant_q(3, 256, 384)
+            multiply(4)
+            invert(3, 0)
+            invert(3, 1)
+            for c in range(SIDE):
+                divide(3, c)
+                store(3, c)
+            quant_q(3, 384, 512)
+            multiply(5)
+            invert(4, 0)
+            invert(4, 1)
+            divide(4, 0)
+            divide(4, 1)
+            store_both(4)
+            invert(5, 0)
+            invert(5, 1)
+            divide(5, 0)
+            divide_on_vector(5, 1)
+            store_both(5)

@@ -19,7 +19,7 @@ ROWS = D // PACK
 SIDE = P // ROWS
 PAIRS = H // SIDE
 M = 128
-RUN = 4
+RUN = 2
 
 
 def tile_rows_read_elu1_norm_kernel(tc, q, qa, S, out):

@@ -14,19 +14,25 @@ ACT = mybir.ActivationFunctionType
 ALU = mybir.AluOpType
 
 P = 128
-PACK = 4
-ROWS = D // PACK
+SLOTS = 4
+ROWS = D // SLOTS
 SIDE = P // ROWS
 PAIRS = H // SIDE
 M = 128
+TILES = N // M
+BANKS = 4
+HALF = N // 2
 RUN = 2
+SPLIT = 288
+
+PIECES = [(0, 0, 2), (1, 0, 4), (2, 0, 4), (3, 0, 2), (3, 2, 2), (0, 2, 1), (0, 3, 1)]
 
 
 def tile_rows_read_elu1_norm_kernel(tc, q, qa, S, out):
     nc = tc.nc
-    q_hbm = q.rearrange("h (p j) n -> (h p) j n", j=PACK)
-    s_hbm = S.rearrange("h (p j) e -> (h p) j e", j=PACK)
-    qa_hbm = qa.rearrange("(p j) o -> p (j o)", j=PACK)
+    q_hbm = q.rearrange("h (p j) n -> (h p) j n", j=SLOTS)
+    s_hbm = S.rearrange("h (p j) e -> (h p) j e", j=SLOTS)
+    qa_hbm = qa.rearrange("(p j) o -> p (j o)", j=SLOTS)
 
     with ExitStack() as ctx:
         sb = ctx.enter_context(tc.tile_pool(name="sb", bufs=1))
@@ -35,67 +41,103 @@ def tile_rows_read_elu1_norm_kernel(tc, q, qa, S, out):
         def per_pair(name, shape, dtype):
             return [sb.tile(shape, dtype, name="%s%d" % (name, g), align_bytes=64) for g in range(PAIRS)]
 
-        q_raw = per_pair("q_raw", [P, PACK, N], F32)
-        q_exp = per_pair("q_exp", [P, PACK, N], F32)
-        low = per_pair("low", [P, PACK, N], F32)
-        high = per_pair("high", [P, PACK, N], F32)
-        fq = per_pair("fq", [P, N, PACK], BF16)
+        q_raw = per_pair("q_raw", [P, SLOTS, N], F32)
+        q_exp = per_pair("q_exp", [P, SLOTS, N], F32)
+        low = per_pair("low", [P, SLOTS, N], F32)
+        high = per_pair("high", [P, SLOTS, N], F32)
+        fq = per_pair("fq", [P, N, SLOTS], BF16)
         q_codes = per_pair("q_codes", [P, N], U32)
         q_scales = per_pair("q_scales", [P, N], U8)
-        s_raw = per_pair("s_raw", [P, PACK, E], F32)
-        s_bf = per_pair("s_bf", [P, E, PACK], BF16)
+        s_raw = per_pair("s_raw", [P, SLOTS, E], F32)
+        s_bf = per_pair("s_bf", [P, E, SLOTS], BF16)
         s_codes = per_pair("s_codes", [P, E], U32)
         s_scales = per_pair("s_scales", [P, E], U8)
-        res = per_pair("res", [P, SIDE, N // M, E], F32)
-        weight = sb.tile([P, PACK], F32, name="weight")
+        res = per_pair("res", [P, SIDE, TILES, E], F32)
+        weight = sb.tile([P, SLOTS], F32, name="weight")
+        below = sb.tile([P, SLOTS, N - SPLIT], F32, name="below")
+        above = sb.tile([P, SLOTS, N - SPLIT], F32, name="above")
         zero = sb.tile([P, 1], F32, name="zero")
-        one = sb.tile([P, 1], F32, name="one")
-        banks = [[psum.tile([P, N // M, E], F32, name="bank%d_%d" % (c, b)) for b in range(4)] for c in range(SIDE)]
+        exp_zero = sb.tile([P, 1], F32, name="exp_zero")
+        inverse = [[sb.tile([P, TILES], F32, name="inverse%d_%d" % (i, c)) for c in range(SIDE)] for i in range(len(PIECES))]
+        banks = [[psum.tile([P, TILES, E], F32, name="bank%d_%d" % (c, b)) for b in range(BANKS)] for c in range(SIDE)]
 
-        pieces = [(0, 0, 4, 0), (1, 0, 4, 1), (2, 0, 4, 2), (3, 0, 2, 3), (3, 2, 1, 0), (3, 3, 1, 1)]
-        inv = [[sb.tile([P, 8], F32, name="inv%d_%d" % (i, c)) for c in range(SIDE)] for i in range(len(pieces))]
+        first_slots, last_slots, all_slots = slice(0, 2), slice(2, SLOTS), slice(0, SLOTS)
+        early, late, whole = slice(0, SPLIT), slice(SPLIT, N), slice(0, N)
 
-        def load_q(g, j0, j1):
-            nc.sync.dma_start(out=q_raw[g][:, j0:j1, :], in_=q_hbm[g * P : (g + 1) * P, j0:j1, :])
+        def load_q(g, slots, cols):
+            nc.sync.dma_start(out=q_raw[g][:, slots, cols], in_=q_hbm[g * P : (g + 1) * P, slots, cols])
 
         def load_s(g):
             nc.sync.dma_start(out=s_raw[g][:], in_=s_hbm[g * P : (g + 1) * P, :, :])
 
-        def exp_q(g, j0, j1):
-            nc.scalar.activation(out=q_exp[g][:, j0:j1, :], in_=q_raw[g][:, j0:j1, :], func=ACT.Exp)
+        def exp_q(g, slots, cols):
+            nc.scalar.activation(out=q_exp[g][:, slots, cols], in_=q_raw[g][:, slots, cols], func=ACT.Exp)
 
-        def make_high(g, j0, j1):
-            nc.vector.tensor_scalar(out=high[g][:, j0:j1, :], in0=q_raw[g][:, j0:j1, :], scalar1=0.0, scalar2=1.0, op0=ALU.max, op1=ALU.add)
+        def make_high(g, slots, cols):
+            nc.vector.tensor_scalar(
+                out=high[g][:, slots, cols], in0=q_raw[g][:, slots, cols], scalar1=0.0, scalar2=1.0, op0=ALU.max, op1=ALU.add
+            )
 
-        def make_low(g, j, n0=0, n1=N):
-            nc.vector.tensor_scalar(out=low[g][:, j, n0:n1], in0=q_exp[g][:, j, n0:n1], scalar1=one[:, 0:1], scalar2=weight[:, j : j + 1], op0=ALU.min, op1=ALU.mult)
+        def make_low(g, j, cols):
+            nc.vector.tensor_scalar(
+                out=low[g][:, j, cols],
+                in0=q_exp[g][:, j, cols],
+                scalar1=exp_zero[:, 0:1],
+                scalar2=weight[:, j : j + 1],
+                op0=ALU.min,
+                op1=ALU.mult,
+            )
 
-        def runs(ap):
-            return ap.rearrange("p j (c i) -> p c j i", i=RUN)
+        def late_below():
+            nc.scalar.activation(out=below[:], in_=q_raw[0][:, :, late], func=ACT.Relu, scale=-1.0)
 
-        def words(ap):
-            return ap.rearrange("p (c i) j -> p c j i", i=RUN)
+        def late_above():
+            nc.scalar.activation(out=above[:], in_=q_raw[0][:, :, late], func=ACT.Relu)
 
-        def product(g, n0, n1):
-            nc.vector.tensor_tensor(out=words(fq[g][:, n0:n1, :]), in0=runs(low[g][:, :, n0:n1]), in1=runs(high[g][:, :, n0:n1]), op=ALU.mult)
+        def late_low():
+            nc.scalar.activation(out=low[0][:, :, late], in_=below[:], func=ACT.Exp, scale=-1.0)
 
-        def quant_q(g, n0, n1):
-            nc.vector.quantize_mx(out=q_codes[g][:, n0:n1].bitcast(FP8X4), scales=q_scales[g][:, n0:n1], in_=fq[g][:, n0:n1, :].rearrange("p n j -> p (n j)"))
+        def late_high():
+            for j in range(SLOTS):
+                w = weight[:, j : j + 1]
+                nc.scalar.activation(out=high[0][:, j, late], in_=above[:, j, :], func=ACT.Identity, scale=w, bias=w)
+
+        def from_slots(ap):
+            return ap.rearrange("p j (k i) -> p k j i", i=RUN)
+
+        def to_words(ap):
+            return ap.rearrange("p (k i) j -> p k j i", i=RUN)
+
+        def columns(i):
+            g, first, count = PIECES[i]
+            return g, slice(first * M, (first + count) * M)
+
+        def product(i):
+            g, cols = columns(i)
+            nc.vector.tensor_tensor(
+                out=to_words(fq[g][:, cols, :]), in0=from_slots(low[g][:, :, cols]), in1=from_slots(high[g][:, :, cols]), op=ALU.mult
+            )
 
         def round_s(g):
-            nc.scalar.copy(out=words(s_bf[g][:]), in_=runs(s_raw[g][:]))
+            nc.scalar.copy(out=to_words(s_bf[g][:]), in_=from_slots(s_raw[g][:]))
 
-        def quant_s(g):
+        def quantise_s(g):
             nc.vector.quantize_mx(out=s_codes[g][:].bitcast(FP8X4), scales=s_scales[g][:], in_=s_bf[g][:].rearrange("p e j -> p (e j)"))
 
+        def quantise_q(i):
+            g, cols = columns(i)
+            nc.vector.quantize_mx(
+                out=q_codes[g][:, cols].bitcast(FP8X4), scales=q_scales[g][:, cols], in_=fq[g][:, cols, :].rearrange("p n j -> p (n j)")
+            )
+
         def multiply(i):
-            g, r0, nr, b = pieces[i]
-            for r in range(nr):
-                cols = slice((r0 + r) * M, (r0 + r + 1) * M)
+            g, first, count = PIECES[i]
+            for r in range(count):
+                cols = slice((first + r) * M, (first + r + 1) * M)
                 for c in range(SIDE):
                     rows = slice(c * ROWS, (c + 1) * ROWS)
                     nc.tensor.matmul_mx(
-                        out=banks[c][b][:, r, :],
+                        out=banks[c][i % BANKS][:, r, :],
                         lhsT=q_codes[g][rows, cols].bitcast(FP8X4),
                         lhsT_scale=q_scales[g][rows, cols],
                         rhs=s_codes[g][rows, :].bitcast(FP8X4),
@@ -105,111 +147,144 @@ def tile_rows_read_elu1_norm_kernel(tc, q, qa, S, out):
                     )
 
         def invert(i, c):
-            g, r0, nr, b = pieces[i]
-            nc.vector.reciprocal(out=inv[i][c][:, 0:nr], in_=banks[c][b][:, 0:nr, E - 1])
+            count = PIECES[i][2]
+            nc.vector.reciprocal(out=inverse[i][c][:, 0:count], in_=banks[c][i % BANKS][:, 0:count, E - 1])
 
-        def divide(i, c):
-            g, r0, nr, b = pieces[i]
-            for r in range(nr):
-                nc.scalar.activation(out=res[g][:, c, r0 + r, :], in_=banks[c][b][:, r, :], func=ACT.Copy, scale=inv[i][c][:, r : r + 1])
+        def divide_on_scalar(i, c):
+            g, first, count = PIECES[i]
+            for r in range(count):
+                nc.scalar.activation(
+                    out=res[g][:, c, first + r, :], in_=banks[c][i % BANKS][:, r, :], func=ACT.Copy, scale=inverse[i][c][:, r : r + 1]
+                )
 
         def divide_on_vector(i, c):
-            g, r0, nr, b = pieces[i]
-            for r in range(nr):
-                nc.vector.tensor_scalar(out=res[g][:, c, r0 + r, :], in0=banks[c][b][:, r, :], scalar1=inv[i][c][:, r : r + 1], scalar2=None, op0=ALU.mult)
+            g, first, count = PIECES[i]
+            nc.vector.tensor_tensor(
+                out=res[g][:, c, first : first + count, :],
+                in0=banks[c][i % BANKS][:, 0:count, :],
+                in1=inverse[i][c][:, 0:count].unsqueeze(2).to_broadcast([P, count, E]),
+                op=ALU.mult,
+            )
 
-        def store(i, c):
-            g, r0, nr, b = pieces[i]
-            dst = out[g * SIDE + c].rearrange("(r s) e -> s r e", s=M)
-            nc.sync.dma_start(out=dst[:, r0 : r0 + nr, :], in_=res[g][:, c, r0 : r0 + nr, :])
+        def store_head(i, c):
+            g, first, count = PIECES[i]
+            head = out[g * SIDE + c].rearrange("(r s) e -> s r e", s=M)
+            nc.sync.dma_start(out=head[:, first : first + count, :], in_=res[g][:, c, first : first + count, :])
 
-        def store_both(i):
-            g, r0, nr, b = pieces[i]
-            dst = out[g * SIDE : (g + 1) * SIDE, r0 * M : (r0 + 1) * M, :].rearrange("c s e -> s c e")
-            nc.sync.dma_start(out=dst, in_=res[g][:, :, r0, :])
+        def store_pair(i):
+            g, cols = columns(i)
+            pair = out[g * SIDE : (g + 1) * SIDE, cols, :].rearrange("c s e -> s c e")
+            nc.sync.dma_start(out=pair, in_=res[g][:, :, PIECES[i][1], :])
+
+        def invert_both(i):
+            for c in range(SIDE):
+                invert(i, c)
+
+        def finish_head(i, c):
+            divide_on_scalar(i, c)
+            store_head(i, c)
+
+        def finish_both(i):
+            for c in range(SIDE):
+                finish_head(i, c)
+
+        def quantise_and_multiply(i):
+            quantise_q(i)
+            multiply(i)
+
+        def make_lows(g):
+            for j in range(SLOTS):
+                make_low(g, j, whole)
 
         with tc.manual_schedule():
+            load_q(0, slice(0, 1), early)
             for c in range(SIDE):
-                nc.scalar.dma_start(out=weight[c * ROWS : (c + 1) * ROWS, :], in_=qa_hbm)
-            for j in range(PACK):
-                load_q(0, j, j + 1)
-            load_q(1, 0, 2)
+                nc.sync.dma_start(out=weight[c * ROWS : (c + 1) * ROWS, :], in_=qa_hbm)
+            for j in range(1, SLOTS):
+                load_q(0, slice(j, j + 1), early)
+            load_q(1, first_slots, whole)
+            load_q(1, last_slots, whole)
             load_s(0)
-            load_q(1, 2, 4)
             load_s(1)
+            load_q(0, all_slots, late)
             for g in (2, 3):
-                load_q(g, 0, 2)
-                load_q(g, 2, 4)
+                load_q(g, first_slots, whole)
+                load_q(g, last_slots, whole)
                 load_s(g)
 
-            nc.vector.memset(zero[:], 0.0)
-            nc.scalar.activation(out=one[:], in_=zero[:], func=ACT.Exp)
+            nc.gpsimd.memset(zero[:], 0.0)
+            nc.scalar.activation(out=exp_zero[:], in_=zero[:], func=ACT.Exp)
 
-            for j in range(PACK):
-                exp_q(0, j, j + 1)
-                make_high(0, j, j + 1)
-                if j < PACK - 1:
-                    make_low(0, j)
-            make_low(0, PACK - 1, 0, N // 2)
-            make_low(0, PACK - 1, N // 2, N)
-            product(0, 0, N // 2)
-            product(0, N // 2, N)
-            exp_q(1, 0, 2)
+            for j in range(SLOTS):
+                exp_q(0, slice(j, j + 1), early)
+            for j in range(SLOTS):
+                make_high(0, slice(j, j + 1), early)
+                if j > 0:
+                    make_low(0, j - 1, early)
+            make_low(0, SLOTS - 1, early)
+            product(0)
+
+            exp_q(1, first_slots, whole)
+            exp_q(1, last_slots, whole)
             round_s(0)
-            exp_q(1, 2, 4)
             round_s(1)
-            make_high(1, 0, 2)
-            quant_q(0, 0, N)
-            make_high(1, 2, 4)
-            quant_s(0)
+            make_high(1, first_slots, whole)
+            make_high(1, last_slots, whole)
+            make_lows(1)
+            quantise_q(0)
+            quantise_s(0)
             multiply(0)
-            for j in range(PACK):
-                make_low(1, j)
-            quant_s(1)
-            invert(0, 0)
-            invert(0, 1)
 
-            for g in (1, 2):
-                product(g, 0, N)
-                exp_q(g + 1, 0, 2)
-                exp_q(g + 1, 2, 4)
-                round_s(g + 1)
-                for c in range(SIDE):
-                    divide(g - 1, c)
-                    store(g - 1, c)
-                make_high(g + 1, 0, 4)
-                quant_q(g, 0, N)
-                multiply(g)
-                for j in range(PACK):
-                    make_low(g + 1, j)
-                quant_s(g + 1)
-                invert(g, 0)
-                invert(g, 1)
+            late_below()
+            exp_q(2, first_slots, whole)
+            exp_q(2, last_slots, whole)
+            product(1)
+            quantise_s(1)
+            invert_both(0)
+            make_high(2, first_slots, whole)
+            quantise_and_multiply(1)
+            make_high(2, last_slots, whole)
+            finish_both(0)
+            round_s(2)
+            make_lows(2)
+            quantise_s(2)
+            invert_both(1)
 
-            product(3, 0, 256)
-            for c in range(SIDE):
-                divide(2, c)
-                store(2, c)
-            product(3, 256, 384)
-            quant_q(3, 0, 256)
-            multiply(3)
-            product(3, 384, 512)
-            quant_q(3, 256, 384)
-            multiply(4)
-            invert(3, 0)
-            invert(3, 1)
-            for c in range(SIDE):
-                divide(3, c)
-                store(3, c)
-            quant_q(3, 384, 512)
-            multiply(5)
-            invert(4, 0)
+            exp_q(3, first_slots, whole)
+            exp_q(3, last_slots, whole)
+            finish_both(1)
+            product(2)
+            make_high(3, first_slots, whole)
+            quantise_and_multiply(2)
+            make_high(3, last_slots, whole)
+            round_s(3)
+            late_above()
+            late_low()
+            late_high()
+            make_lows(3)
+            quantise_s(3)
+            invert_both(2)
+            finish_both(2)
+
+            product(3)
+            product(4)
+            quantise_and_multiply(3)
+            product(5)
+            quantise_and_multiply(4)
+            invert_both(3)
+            finish_both(3)
+            product(6)
+
+            quantise_and_multiply(5)
             invert(4, 1)
-            divide(4, 0)
-            divide(4, 1)
-            store_both(4)
-            invert(5, 0)
-            invert(5, 1)
-            divide(5, 0)
-            divide_on_vector(5, 1)
-            store_both(5)
+            quantise_and_multiply(6)
+            invert(4, 0)
+            divide_on_vector(4, 1)
+            store_head(4, 1)
+            finish_head(4, 0)
+            invert_both(5)
+            invert_both(6)
+            for i in (5, 6):
+                divide_on_scalar(i, 0)
+                divide_on_vector(i, 1)
+                store_pair(i)

from contextlib import ExitStack

import concourse.mybir as mybir

H, D, N, E = 8, 256, 512, 128
FLOPS = 2 * H * N * D * E

F32 = mybir.dt.float32
BF16 = mybir.dt.bfloat16
U32 = mybir.dt.uint32
U8 = mybir.dt.uint8
FP8X4 = mybir.dt.float8_e4m3fn_x4
ACT = mybir.ActivationFunctionType
ALU = mybir.AluOpType

P = 128
SLOTS = 4
ROWS = D // SLOTS
SIDE = P // ROWS
PAIRS = H // SIDE
M = 128
TILES = N // M
BANKS = 4
HALF = N // 2
RUN = 2
SPLIT = 288

PIECES = [(0, 0, 2), (1, 0, 4), (2, 0, 4), (3, 0, 2), (3, 2, 2), (0, 2, 1), (0, 3, 1)]


def tile_rows_read_elu1_norm_kernel(tc, q, qa, S, out):
    nc = tc.nc
    q_hbm = q.rearrange("h (p j) n -> (h p) j n", j=SLOTS)
    s_hbm = S.rearrange("h (p j) e -> (h p) j e", j=SLOTS)
    qa_hbm = qa.rearrange("(p j) o -> p (j o)", j=SLOTS)

    with ExitStack() as ctx:
        sb = ctx.enter_context(tc.tile_pool(name="sb", bufs=1))
        psum = ctx.enter_context(tc.psum_pool(name="psum", bufs=1))

        def per_pair(name, shape, dtype):
            return [sb.tile(shape, dtype, name="%s%d" % (name, g), align_bytes=64) for g in range(PAIRS)]

        q_raw = per_pair("q_raw", [P, SLOTS, N], F32)
        q_exp = per_pair("q_exp", [P, SLOTS, N], F32)
        low = per_pair("low", [P, SLOTS, N], F32)
        high = per_pair("high", [P, SLOTS, N], F32)
        fq = per_pair("fq", [P, N, SLOTS], BF16)
        q_codes = per_pair("q_codes", [P, N], U32)
        q_scales = per_pair("q_scales", [P, N], U8)
        s_raw = per_pair("s_raw", [P, SLOTS, E], F32)
        s_bf = per_pair("s_bf", [P, E, SLOTS], BF16)
        s_codes = per_pair("s_codes", [P, E], U32)
        s_scales = per_pair("s_scales", [P, E], U8)
        res = per_pair("res", [P, SIDE, TILES, E], F32)
        weight = sb.tile([P, SLOTS], F32, name="weight")
        below = sb.tile([P, SLOTS, N - SPLIT], F32, name="below")
        above = sb.tile([P, SLOTS, N - SPLIT], F32, name="above")
        zero = sb.tile([P, 1], F32, name="zero")
        exp_zero = sb.tile([P, 1], F32, name="exp_zero")
        inverse = [[sb.tile([P, TILES], F32, name="inverse%d_%d" % (i, c)) for c in range(SIDE)] for i in range(len(PIECES))]
        banks = [[psum.tile([P, TILES, E], F32, name="bank%d_%d" % (c, b)) for b in range(BANKS)] for c in range(SIDE)]

        first_slots, last_slots, all_slots = slice(0, 2), slice(2, SLOTS), slice(0, SLOTS)
        early, late, whole = slice(0, SPLIT), slice(SPLIT, N), slice(0, N)

        def load_q(g, slots, cols):
            nc.sync.dma_start(out=q_raw[g][:, slots, cols], in_=q_hbm[g * P : (g + 1) * P, slots, cols])

        def load_s(g):
            nc.sync.dma_start(out=s_raw[g][:], in_=s_hbm[g * P : (g + 1) * P, :, :])

        def exp_q(g, slots, cols):
            nc.scalar.activation(out=q_exp[g][:, slots, cols], in_=q_raw[g][:, slots, cols], func=ACT.Exp)

        def make_high(g, slots, cols):
            nc.vector.tensor_scalar(
                out=high[g][:, slots, cols], in0=q_raw[g][:, slots, cols], scalar1=0.0, scalar2=1.0, op0=ALU.max, op1=ALU.add
            )

        def make_low(g, j, cols):
            nc.vector.tensor_scalar(
                out=low[g][:, j, cols],
                in0=q_exp[g][:, j, cols],
                scalar1=exp_zero[:, 0:1],
                scalar2=weight[:, j : j + 1],
                op0=ALU.min,
                op1=ALU.mult,
            )

        def late_below():
            nc.scalar.activation(out=below[:], in_=q_raw[0][:, :, late], func=ACT.Relu, scale=-1.0)

        def late_above():
            nc.scalar.activation(out=above[:], in_=q_raw[0][:, :, late], func=ACT.Relu)

        def late_low():
            nc.scalar.activation(out=low[0][:, :, late], in_=below[:], func=ACT.Exp, scale=-1.0)

        def late_high():
            for j in range(SLOTS):
                w = weight[:, j : j + 1]
                nc.scalar.activation(out=high[0][:, j, late], in_=above[:, j, :], func=ACT.Identity, scale=w, bias=w)

        def from_slots(ap):
            return ap.rearrange("p j (k i) -> p k j i", i=RUN)

        def to_words(ap):
            return ap.rearrange("p (k i) j -> p k j i", i=RUN)

        def columns(i):
            g, first, count = PIECES[i]
            return g, slice(first * M, (first + count) * M)

        def product(i):
            g, cols = columns(i)
            nc.vector.tensor_tensor(
                out=to_words(fq[g][:, cols, :]), in0=from_slots(low[g][:, :, cols]), in1=from_slots(high[g][:, :, cols]), op=ALU.mult
            )

        def round_s(g):
            nc.scalar.copy(out=to_words(s_bf[g][:]), in_=from_slots(s_raw[g][:]))

        def quantise_s(g):
            nc.vector.quantize_mx(out=s_codes[g][:].bitcast(FP8X4), scales=s_scales[g][:], in_=s_bf[g][:].rearrange("p e j -> p (e j)"))

        def quantise_q(i):
            g, cols = columns(i)
            nc.vector.quantize_mx(
                out=q_codes[g][:, cols].bitcast(FP8X4), scales=q_scales[g][:, cols], in_=fq[g][:, cols, :].rearrange("p n j -> p (n j)")
            )

        def multiply(i):
            g, first, count = PIECES[i]
            for r in range(count):
                cols = slice((first + r) * M, (first + r + 1) * M)
                for c in range(SIDE):
                    rows = slice(c * ROWS, (c + 1) * ROWS)
                    nc.tensor.matmul_mx(
                        out=banks[c][i % BANKS][:, r, :],
                        lhsT=q_codes[g][rows, cols].bitcast(FP8X4),
                        lhsT_scale=q_scales[g][rows, cols],
                        rhs=s_codes[g][rows, :].bitcast(FP8X4),
                        rhs_scale=s_scales[g][rows, :],
                        start=True,
                        stop=True,
                    )

        def invert(i, c):
            count = PIECES[i][2]
            nc.vector.reciprocal(out=inverse[i][c][:, 0:count], in_=banks[c][i % BANKS][:, 0:count, E - 1])

        def divide_on_scalar(i, c):
            g, first, count = PIECES[i]
            for r in range(count):
                nc.scalar.activation(
                    out=res[g][:, c, first + r, :], in_=banks[c][i % BANKS][:, r, :], func=ACT.Copy, scale=inverse[i][c][:, r : r + 1]
                )

        def divide_on_vector(i, c):
            g, first, count = PIECES[i]
            nc.vector.tensor_tensor(
                out=res[g][:, c, first : first + count, :],
                in0=banks[c][i % BANKS][:, 0:count, :],
                in1=inverse[i][c][:, 0:count].unsqueeze(2).to_broadcast([P, count, E]),
                op=ALU.mult,
            )

        def store_head(i, c):
            g, first, count = PIECES[i]
            head = out[g * SIDE + c].rearrange("(r s) e -> s r e", s=M)
            nc.sync.dma_start(out=head[:, first : first + count, :], in_=res[g][:, c, first : first + count, :])

        def store_pair(i):
            g, cols = columns(i)
            pair = out[g * SIDE : (g + 1) * SIDE, cols, :].rearrange("c s e -> s c e")
            nc.sync.dma_start(out=pair, in_=res[g][:, :, PIECES[i][1], :])

        def invert_both(i):
            for c in range(SIDE):
                invert(i, c)

        def finish_head(i, c):
            divide_on_scalar(i, c)
            store_head(i, c)

        def finish_both(i):
            for c in range(SIDE):
                finish_head(i, c)

        def quantise_and_multiply(i):
            quantise_q(i)
            multiply(i)

        def make_lows(g):
            for j in range(SLOTS):
                make_low(g, j, whole)

        with tc.manual_schedule():
            load_q(0, slice(0, 1), early)
            for c in range(SIDE):
                nc.sync.dma_start(out=weight[c * ROWS : (c + 1) * ROWS, :], in_=qa_hbm)
            for j in range(1, SLOTS):
                load_q(0, slice(j, j + 1), early)
            load_q(1, first_slots, whole)
            load_q(1, last_slots, whole)
            load_s(0)
            load_s(1)
            load_q(0, all_slots, late)
            for g in (2, 3):
                load_q(g, first_slots, whole)
                load_q(g, last_slots, whole)
                load_s(g)

            nc.gpsimd.memset(zero[:], 0.0)
            nc.scalar.activation(out=exp_zero[:], in_=zero[:], func=ACT.Exp)

            for j in range(SLOTS):
                exp_q(0, slice(j, j + 1), early)
            for j in range(SLOTS):
                make_high(0, slice(j, j + 1), early)
                if j > 0:
                    make_low(0, j - 1, early)
            make_low(0, SLOTS - 1, early)
            product(0)

            exp_q(1, first_slots, whole)
            exp_q(1, last_slots, whole)
            round_s(0)
            round_s(1)
            make_high(1, first_slots, whole)
            make_high(1, last_slots, whole)
            make_lows(1)
            quantise_q(0)
            quantise_s(0)
            multiply(0)

            late_below()
            exp_q(2, first_slots, whole)
            exp_q(2, last_slots, whole)
            product(1)
            quantise_s(1)
            invert_both(0)
            make_high(2, first_slots, whole)
            quantise_and_multiply(1)
            make_high(2, last_slots, whole)
            finish_both(0)
            round_s(2)
            make_lows(2)
            quantise_s(2)
            invert_both(1)

            exp_q(3, first_slots, whole)
            exp_q(3, last_slots, whole)
            finish_both(1)
            product(2)
            make_high(3, first_slots, whole)
            quantise_and_multiply(2)
            make_high(3, last_slots, whole)
            round_s(3)
            late_above()
            late_low()
            late_high()
            make_lows(3)
            quantise_s(3)
            invert_both(2)
            finish_both(2)

            product(3)
            product(4)
            quantise_and_multiply(3)
            product(5)
            quantise_and_multiply(4)
            invert_both(3)
            finish_both(3)
            product(6)

            quantise_and_multiply(5)
            invert(4, 1)
            quantise_and_multiply(6)
            invert(4, 0)
            divide_on_vector(4, 1)
            store_head(4, 1)
            finish_head(4, 0)
            invert_both(5)
            invert_both(6)
            for i in (5, 6):
                divide_on_scalar(i, 0)
                divide_on_vector(i, 1)
                store_pair(i)
